import numpy as np
import ml_dtypes


def mxq(x, axis, fmt="e4m3"):
    dtype, down = {"e4m3": (ml_dtypes.float8_e4m3fn, 7), "e5m2": (ml_dtypes.float8_e5m2, 14)}[fmt]
    v = np.moveaxis(np.asarray(x, np.float32).astype(ml_dtypes.bfloat16).astype(np.float64), axis, -1)
    blocks = v.reshape(v.shape[:-1] + (-1, 32))
    amax = np.abs(blocks).max(-1, keepdims=True)
    byte = np.maximum(np.where(amax > 0, np.frexp(amax)[1] - 1 + 127, 0) - down, 1)
    scale = np.exp2(byte - 127.0)
    codes = (blocks / scale).astype(np.float32).astype(dtype).astype(np.float64)
    return np.moveaxis((codes * scale).reshape(v.shape), -1, axis)


WIDE = False


def mx_kscale(k):
    if not WIDE:
        return np.ones(k)
    levels = np.array([10, -10, 5, -5, 0])
    if k % 512:
        return np.exp2(np.random.permutation(np.resize(levels, k // 32))).repeat(32)
    a = np.empty((k // 512, 16))
    for p in range(k // 512):
        a[p, :8] = np.random.permutation(np.resize(levels, 8))
        for g in range(8):
            far = levels[np.abs(levels - a[p, g]) >= 10]
            a[p, g + 8] = far[np.random.randint(len(far))]
    return np.exp2(a.ravel()).repeat(32)


def f64(x):
    return np.asarray(x).astype(np.float64)


def striped8(idx):
    return np.asarray(idx).reshape(8, -1, 16).transpose(0, 2, 1).reshape(128, -1).astype(np.uint16)


def unstriped8(offs):
    return offs.reshape(8, 16, -1).transpose(0, 2, 1).reshape(8, -1).astype(np.int64)


def pick8(x, idx, run):
    r = np.arange(len(x))
    return x[r[:, None], idx[r % (8 * run) // run]]


E2M1 = np.array([0.0, 0.5, 1.0, 1.5, 2.0, 3.0, 4.0, 6.0, -0.0, -0.5, -1.0, -1.5, -2.0, -3.0, -4.0, -6.0])


def pack_weight(w, fmt):
    k, n = w.shape
    w = f64(np.asarray(w, np.float32).astype(ml_dtypes.bfloat16)).reshape(k // 32, 32, n)
    amax = np.abs(w).max(1)
    if fmt == "e4m3":
        byte = np.frexp(amax)[1] - 1 + 127 - 7
    else:
        mant, ex = np.frexp(amax / 6.0)
        byte = np.where(mant > 0.5, ex, ex - 1) + 127
    byte = np.clip(np.where(amax > 0, byte, 1), 1, 254)
    scaled = (w * np.exp2(127.0 - byte)[:, None, :]).reshape(k, n).astype(np.float32)
    by_word = np.ascontiguousarray(scaled.reshape(k // 512, 128, 4, n).transpose(0, 1, 3, 2))
    if fmt == "e4m3":
        words = by_word.astype(ml_dtypes.float8_e4m3fn).view(np.uint8)
    else:
        c = by_word.astype(ml_dtypes.float4_e2m1fn).view(np.uint8) & 0xF
        words = (c[..., 0::2] | (c[..., 1::2] << 4)).reshape(k // 512, 128, 2 * n)
    return np.ascontiguousarray(words), np.ascontiguousarray(byte.astype(np.uint8).reshape(k // 512, 16, n))


def unpack_weight(words, scales, fmt):
    g, _, n = scales.shape
    words = np.ascontiguousarray(words).reshape(g, 128, n, -1)
    if fmt == "e4m3":
        vals = words.view(ml_dtypes.float8_e4m3fn).astype(np.float64)
    else:
        nib = np.empty((g, 128, n, 4), np.uint8)
        nib[..., 0::2] = words & 0xF
        nib[..., 1::2] = words >> 4
        vals = E2M1[nib]
    vals = vals * np.repeat(np.exp2(scales.astype(np.float64) - 127.0), 8, axis=1)[..., None]
    return vals.transpose(0, 1, 3, 2).reshape(g * 512, n)


def sigmoid(v):
    return 1.0 / (1.0 + np.exp(-v))


D, T, U, I, Q = 512, 1024, 1024, 512, 128


def setup_inputs():
    n = np.random.standard_normal
    idx = np.stack([np.random.permutation(T)[:I] for _ in range(8)])
    idx2 = np.stack([np.random.permutation(U)[:I] for _ in range(8)])
    idx3 = np.stack([np.random.permutation(T)[:I] for _ in range(8)])
    idx4 = np.stack([np.random.permutation(T)[:I] for _ in range(8)])
    idx5 = np.stack([np.random.permutation(U)[:I] for _ in range(8)])
    fd = mx_kscale(D)
    keysp = pack_weight(n((D, T)) / fd[:, None], "e4m3")
    notesp = pack_weight(n((D, U)) / fd[:, None], "e2m1")
    return {
        "query": (n((D, Q)) * 1.0 / np.sqrt(D) * fd[:, None]).astype(np.float32),
        "keys_words": keysp[0],
        "keys_scales": keysp[1],
        "notes_words": notesp[0],
        "notes_scales": notesp[1],
        "thr": (np.random.uniform(-0.6, 0.6, (Q, 1))).astype(np.float32),
        "slope": (np.random.uniform(0.8, 2.0, (Q, 1))).astype(np.float32),
        "offs": striped8(idx),
        "offs2": striped8(idx2),
        "offs3": striped8(idx3),
        "offs4": striped8(idx4),
        "offs5": striped8(idx5),
    }


def reference(query, keys_words, keys_scales, notes_words, notes_scales, thr, slope, offs, offs2, offs3, offs4, offs5):
    idx = unstriped8(offs)
    idx2 = unstriped8(offs2)
    idx3 = unstriped8(offs3)
    idx4 = unstriped8(offs4)
    idx5 = unstriped8(offs5)
    keysu = unpack_weight(keys_words, keys_scales, "e4m3")
    notesu = unpack_weight(notes_words, notes_scales, "e2m1")
    queryq = mxq(f64(query), 0, "e4m3")
    a = queryq.T @ keysu
    b = queryq.T @ notesu
    s1 = sigmoid(pick8(a, idx, 16) * f64(slope) + f64(thr))
    w = pick8(b, idx2, 16) * s1
    f1 = np.zeros((Q, T))
    f1[np.arange(Q)[:, None], idx3[np.arange(Q) % 128 // 16]] = w
    aa = a + f1
    s2 = sigmoid(pick8(aa, idx4, 16) * f64(slope) + f64(thr))
    y = pick8(b, idx5, 16) - s2 * 2.0
    return y

@@ -1,0 +1,146 @@
+from contextlib import ExitStack
+
+import concourse.mybir as mybir
+
+D, T, U, I, Q = 512, 1024, 1024, 512, 128
+FLOPS = 2 * D * Q * (T + U)
+
+F32 = mybir.dt.float32
+BF16 = mybir.dt.bfloat16
+I32 = mybir.dt.int32
+U32 = mybir.dt.uint32
+U16 = mybir.dt.uint16
+U8 = mybir.dt.uint8
+FP8X4 = mybir.dt.float8_e4m3fn_x4
+FP4X4 = mybir.dt.float4_e2m1fn_x4
+ALU = mybir.AluOpType
+ACT = mybir.ActivationFunctionType
+
+P = 128
+PACK = 4
+BANK = 512
+HALF = I // 2
+GROUP = 16
+N_PASS = 256
+CAST_SPLIT = 88
+ADD_SPLIT = 704
+
+
+def tile_attend_twodoors_two_kernel(
+    tc, query, keys_words, keys_scales, notes_words, notes_scales, thr, slope, offs, offs2, offs3, offs4, offs5, out
+):
+    nc = tc.nc
+    with ExitStack() as ctx:
+        sb = ctx.enter_context(tc.tile_pool(name="sb", bufs=1))
+        psum = ctx.enter_context(tc.psum_pool(name="psum", bufs=1))
+
+        key_planes = sb.tile([P, BANK], U8, align_bytes=64)
+        note_plane = sb.tile([P, U], U8, align_bytes=64)
+        f1 = sb.tile([P, T], F32)
+        nc.vector.memset(key_planes[:].bitcast(I32), 0)
+        nc.vector.memset(note_plane[:].bitcast(I32), 0)
+        nc.vector.memset(f1[:], 0.0)
+
+        q_raw = sb.tile([P, PACK, Q], F32)
+        nc.sync.dma_start(out=q_raw[:], in_=query.rearrange("(p j) q -> p j q", j=PACK))
+        for quad in range(4):
+            rows = keys_scales[0, 4 * quad : 4 * quad + 4, :].bitcast(I32)
+            nc.sync.dma_start(
+                out=key_planes[32 * quad + 4 : 32 * quad + 12, :].bitcast(I32),
+                in_=rows.rearrange("r (h c) -> h r c", h=2),
+            )
+        key_codes = sb.tile([P, T], I32, align_bytes=64)
+        key_words = keys_words[0].rearrange("p n t -> p (n t)").bitcast(I32)
+        for h in range(2):
+            nc.sync.dma_start(out=key_codes[:, h * BANK : (h + 1) * BANK], in_=key_words[:, h * BANK : (h + 1) * BANK])
+        note_codes = sb.tile([P, 2 * U], U8, align_bytes=64)
+        nc.sync.dma_start(out=note_codes[:].bitcast(I32), in_=notes_words[0].bitcast(I32))
+        for quad in range(4):
+            nc.sync.dma_start(
+                out=note_plane[32 * quad : 32 * quad + 4, :].bitcast(I32),
+                in_=notes_scales[0, 4 * quad : 4 * quad + 4, :].bitcast(I32),
+            )
+        slope_sb = sb.tile([P, 1], F32)
+        thr_sb = sb.tile([P, 1], F32)
+        nc.sync.dma_start(out=slope_sb[:], in_=slope)
+        nc.gpsimd.dma_start(out=thr_sb[:], in_=thr)
+        lists = {}
+        for name, src in (("offs", offs), ("offs2", offs2), ("offs3", offs3), ("offs5", offs5), ("offs4", offs4)):
+            lists[name] = sb.tile([P, I // GROUP], U16, name=name + "_sb")
+            nc.sync.dma_start(lists[name][:], src)
+
+        def half_list(name, h):
+            return lists[name][:, h * HALF // GROUP : (h + 1) * HALF // GROUP]
+
+        q_bf = sb.tile([P, Q, PACK], BF16, align_bytes=64)
+        cast_in = q_raw[:].rearrange("p j (c i) -> p c j i", i=4)
+        cast_out = q_bf[:].rearrange("p (c i) j -> p c j i", i=4)
+        nc.vector.tensor_copy(out=cast_out[:, : CAST_SPLIT // 4], in_=cast_in[:, : CAST_SPLIT // 4])
+        nc.scalar.copy(out=cast_out[:, CAST_SPLIT // 4 :], in_=cast_in[:, CAST_SPLIT // 4 :])
+        q_codes = sb.tile([P, Q], U32, align_bytes=64)
+        q_plane = sb.tile([P, Q], U8, align_bytes=64)
+        nc.vector.quantize_mx(
+            out=q_codes[:].bitcast(FP8X4), scales=q_plane[:], in_=q_bf[:].rearrange("p q j -> p (q j)")
+        )
+
+        a = sb.tile([P, T], F32)
+        b = sb.tile([P, U], F32)
+        a_banks = []
+        for n in range(T // N_PASS):
+            cols = slice(n * N_PASS, (n + 1) * N_PASS)
+            h, first = divmod(n * N_PASS, BANK)
+            bank = psum.tile([P, N_PASS], F32, name="a_bank%d" % n)
+            nc.tensor.matmul_mx(
+                out=bank[:],
+                lhsT=q_codes[:].bitcast(FP8X4),
+                lhsT_scale=q_plane[:],
+                rhs=key_codes[:, cols].bitcast(FP8X4),
+                rhs_scale=key_planes[4 + 4 * h : P, first : first + N_PASS],
+                start=True,
+                stop=True,
+            )
+            if n % 2 == 0:
+                nc.scalar.copy(out=a[:, cols], in_=bank[:])
+            else:
+                nc.vector.tensor_copy(out=a[:, cols], in_=bank[:])
+            a_banks.append(bank)
+        for n in range(U // N_PASS):
+            cols = slice(n * N_PASS, (n + 1) * N_PASS)
+            bank = psum.tile([P, N_PASS], F32, name="b_bank%d" % n)
+            nc.tensor.matmul_mx(
+                out=bank[:],
+                lhsT=q_codes[:].bitcast(FP8X4),
+                lhsT_scale=q_plane[:],
+                rhs=note_codes[:, 2 * n * N_PASS : 2 * (n + 1) * N_PASS].bitcast(FP4X4),
+                rhs_scale=note_plane[:, cols],
+                start=True,
+                stop=True,
+            )
+            nc.vector.tensor_copy(out=b[:, cols], in_=bank[:])
+
+        s1 = sb.tile([P, I], F32)
+        b2 = sb.tile([P, I], F32)
+        nc.scalar.activation(s1[:], a[:].indirect(lists["offs"][:]), ACT.Sigmoid, bias=thr_sb[:], scale=slope_sb[:])
+        nc.vector.tensor_copy(b2[:, :HALF], b[:].indirect(half_list("offs2", 0)))
+        nc.scalar.activation(b2[:, HALF:], b[:].indirect(half_list("offs2", 1)), ACT.Copy)
+        nc.vector.tensor_tensor(f1[:].indirect(lists["offs3"][:]), b2[:], s1[:], ALU.mult)
+        b5 = sb.tile([P, I], F32)
+        nc.scalar.activation(b5[:], b[:].indirect(lists["offs5"][:]), ACT.Copy)
+
+        aa = sb.tile([P, T], F32)
+        nc.gpsimd.tensor_tensor(aa[:, ADD_SPLIT:], a[:, ADD_SPLIT:], f1[:, ADD_SPLIT:], ALU.add)
+        for first in range(0, ADD_SPLIT, N_PASS):
+            width = min(N_PASS, ADD_SPLIT - first)
+            cols = slice(first, first + width)
+            nc.vector.tensor_tensor(aa[:, cols], a_banks[first // N_PASS][:, :width], f1[:, cols], ALU.add)
+        for h in range(2):
+            s2 = sb.tile([P, HALF], F32, name="s2_%d" % h)
+            nc.scalar.activation(
+                s2[:], aa[:].indirect(half_list("offs4", h)), ACT.Sigmoid, bias=thr_sb[:], scale=slope_sb[:]
+            )
+            pieces = [(0, HALF, nc.sync)] if h == 0 else [(0, HALF // 2, nc.sync), (HALF // 2, HALF, nc.scalar)]
+            for lo, hi, queue in pieces:
+                cols = slice(h * HALF + lo, h * HALF + hi)
+                y = sb.tile([P, hi - lo], F32, name="y_%d_%d" % (h, lo))
+                nc.vector.scalar_tensor_tensor(y[:], s2[:, lo:hi], -2.0, b5[:, cols], ALU.mult, ALU.add)
+                queue.dma_start(out=out[:, cols], in_=y[:])

@@ -69,6 +69,11 @@ def tile_attend_twodoors_two_kernel(
             lists[name] = sb.tile([P, I // GROUP], U16, name=name + "_sb")
             nc.sync.dma_start(lists[name][:], src)
 
+        warm_in = sb.tile([P, 1], F32)
+        warm_out = sb.tile([P, 1], F32)
+        nc.vector.memset(warm_in[:], 0.0)
+        nc.scalar.activation(warm_out[:], warm_in[:], ACT.Sigmoid)
+
         def half_list(name, h):
             return lists[name][:, h * HALF // GROUP : (h + 1) * HALF // GROUP]
 

from contextlib import ExitStack

import concourse.mybir as mybir

D, T, U, I, Q = 512, 1024, 1024, 512, 128
FLOPS = 2 * D * Q * (T + U)

F32 = mybir.dt.float32
BF16 = mybir.dt.bfloat16
I32 = mybir.dt.int32
U32 = mybir.dt.uint32
U16 = mybir.dt.uint16
U8 = mybir.dt.uint8
FP8X4 = mybir.dt.float8_e4m3fn_x4
FP4X4 = mybir.dt.float4_e2m1fn_x4
ALU = mybir.AluOpType
ACT = mybir.ActivationFunctionType

P = 128
PACK = 4
BANK = 512
HALF = I // 2
GROUP = 16
N_PASS = 256
CAST_SPLIT = 88
ADD_SPLIT = 704


def tile_attend_twodoors_two_kernel(
    tc, query, keys_words, keys_scales, notes_words, notes_scales, thr, slope, offs, offs2, offs3, offs4, offs5, out
):
    nc = tc.nc
    with ExitStack() as ctx:
        sb = ctx.enter_context(tc.tile_pool(name="sb", bufs=1))
        psum = ctx.enter_context(tc.psum_pool(name="psum", bufs=1))

        key_planes = sb.tile([P, BANK], U8, align_bytes=64)
        note_plane = sb.tile([P, U], U8, align_bytes=64)
        f1 = sb.tile([P, T], F32)
        nc.vector.memset(key_planes[:].bitcast(I32), 0)
        nc.vector.memset(note_plane[:].bitcast(I32), 0)
        nc.vector.memset(f1[:], 0.0)

        q_raw = sb.tile([P, PACK, Q], F32)
        nc.sync.dma_start(out=q_raw[:], in_=query.rearrange("(p j) q -> p j q", j=PACK))
        for quad in range(4):
            rows = keys_scales[0, 4 * quad : 4 * quad + 4, :].bitcast(I32)
            nc.sync.dma_start(
                out=key_planes[32 * quad + 4 : 32 * quad + 12, :].bitcast(I32),
                in_=rows.rearrange("r (h c) -> h r c", h=2),
            )
        key_codes = sb.tile([P, T], I32, align_bytes=64)
        key_words = keys_words[0].rearrange("p n t -> p (n t)").bitcast(I32)
        for h in range(2):
            nc.sync.dma_start(out=key_codes[:, h * BANK : (h + 1) * BANK], in_=key_words[:, h * BANK : (h + 1) * BANK])
        note_codes = sb.tile([P, 2 * U], U8, align_bytes=64)
        nc.sync.dma_start(out=note_codes[:].bitcast(I32), in_=notes_words[0].bitcast(I32))
        for quad in range(4):
            nc.sync.dma_start(
                out=note_plane[32 * quad : 32 * quad + 4, :].bitcast(I32),
                in_=notes_scales[0, 4 * quad : 4 * quad + 4, :].bitcast(I32),
            )
        slope_sb = sb.tile([P, 1], F32)
        thr_sb = sb.tile([P, 1], F32)
        nc.sync.dma_start(out=slope_sb[:], in_=slope)
        nc.gpsimd.dma_start(out=thr_sb[:], in_=thr)
        lists = {}
        for name, src in (("offs", offs), ("offs2", offs2), ("offs3", offs3), ("offs5", offs5), ("offs4", offs4)):
            lists[name] = sb.tile([P, I // GROUP], U16, name=name + "_sb")
            nc.sync.dma_start(lists[name][:], src)

        warm_in = sb.tile([P, 1], F32)
        warm_out = sb.tile([P, 1], F32)
        nc.vector.memset(warm_in[:], 0.0)
        nc.scalar.activation(warm_out[:], warm_in[:], ACT.Sigmoid)

        def half_list(name, h):
            return lists[name][:, h * HALF // GROUP : (h + 1) * HALF // GROUP]

        q_bf = sb.tile([P, Q, PACK], BF16, align_bytes=64)
        cast_in = q_raw[:].rearrange("p j (c i) -> p c j i", i=4)
        cast_out = q_bf[:].rearrange("p (c i) j -> p c j i", i=4)
        nc.vector.tensor_copy(out=cast_out[:, : CAST_SPLIT // 4], in_=cast_in[:, : CAST_SPLIT // 4])
        nc.scalar.copy(out=cast_out[:, CAST_SPLIT // 4 :], in_=cast_in[:, CAST_SPLIT // 4 :])
        q_codes = sb.tile([P, Q], U32, align_bytes=64)
        q_plane = sb.tile([P, Q], U8, align_bytes=64)
        nc.vector.quantize_mx(
            out=q_codes[:].bitcast(FP8X4), scales=q_plane[:], in_=q_bf[:].rearrange("p q j -> p (q j)")
        )

        a = sb.tile([P, T], F32)
        b = sb.tile([P, U], F32)
        a_banks = []
        for n in range(T // N_PASS):
            cols = slice(n * N_PASS, (n + 1) * N_PASS)
            h, first = divmod(n * N_PASS, BANK)
            bank = psum.tile([P, N_PASS], F32, name="a_bank%d" % n)
            nc.tensor.matmul_mx(
                out=bank[:],
                lhsT=q_codes[:].bitcast(FP8X4),
                lhsT_scale=q_plane[:],
                rhs=key_codes[:, cols].bitcast(FP8X4),
                rhs_scale=key_planes[4 + 4 * h : P, first : first + N_PASS],
                start=True,
                stop=True,
            )
            if n % 2 == 0:
                nc.scalar.copy(out=a[:, cols], in_=bank[:])
            else:
                nc.vector.tensor_copy(out=a[:, cols], in_=bank[:])
            a_banks.append(bank)
        for n in range(U // N_PASS):
            cols = slice(n * N_PASS, (n + 1) * N_PASS)
            bank = psum.tile([P, N_PASS], F32, name="b_bank%d" % n)
            nc.tensor.matmul_mx(
                out=bank[:],
                lhsT=q_codes[:].bitcast(FP8X4),
                lhsT_scale=q_plane[:],
                rhs=note_codes[:, 2 * n * N_PASS : 2 * (n + 1) * N_PASS].bitcast(FP4X4),
                rhs_scale=note_plane[:, cols],
                start=True,
                stop=True,
            )
            nc.vector.tensor_copy(out=b[:, cols], in_=bank[:])

        s1 = sb.tile([P, I], F32)
        b2 = sb.tile([P, I], F32)
        nc.scalar.activation(s1[:], a[:].indirect(lists["offs"][:]), ACT.Sigmoid, bias=thr_sb[:], scale=slope_sb[:])
        nc.vector.tensor_copy(b2[:, :HALF], b[:].indirect(half_list("offs2", 0)))
        nc.scalar.activation(b2[:, HALF:], b[:].indirect(half_list("offs2", 1)), ACT.Copy)
        nc.vector.tensor_tensor(f1[:].indirect(lists["offs3"][:]), b2[:], s1[:], ALU.mult)
        b5 = sb.tile([P, I], F32)
        nc.scalar.activation(b5[:], b[:].indirect(lists["offs5"][:]), ACT.Copy)

        aa = sb.tile([P, T], F32)
        nc.gpsimd.tensor_tensor(aa[:, ADD_SPLIT:], a[:, ADD_SPLIT:], f1[:, ADD_SPLIT:], ALU.add)
        for first in range(0, ADD_SPLIT, N_PASS):
            width = min(N_PASS, ADD_SPLIT - first)
            cols = slice(first, first + width)
            nc.vector.tensor_tensor(aa[:, cols], a_banks[first // N_PASS][:, :width], f1[:, cols], ALU.add)
        for h in range(2):
            s2 = sb.tile([P, HALF], F32, name="s2_%d" % h)
            nc.scalar.activation(
                s2[:], aa[:].indirect(half_list("offs4", h)), ACT.Sigmoid, bias=thr_sb[:], scale=slope_sb[:]
            )
            pieces = [(0, HALF, nc.sync)] if h == 0 else [(0, HALF // 2, nc.sync), (HALF // 2, HALF, nc.scalar)]
            for lo, hi, queue in pieces:
                cols = slice(h * HALF + lo, h * HALF + hi)
                y = sb.tile([P, hi - lo], F32, name="y_%d_%d" % (h, lo))
                nc.vector.scalar_tensor_tensor(y[:], s2[:, lo:hi], -2.0, b5[:, cols], ALU.mult, ALU.add)
                queue.dma_start(out=out[:, cols], in_=y[:])
